import numpy as np
import ml_dtypes


def mxq(x, axis, fmt="e4m3"):
    dtype, down = {"e4m3": (ml_dtypes.float8_e4m3fn, 7), "e5m2": (ml_dtypes.float8_e5m2, 14)}[fmt]
    v = np.moveaxis(np.asarray(x, np.float32).astype(ml_dtypes.bfloat16).astype(np.float64), axis, -1)
    blocks = v.reshape(v.shape[:-1] + (-1, 32))
    amax = np.abs(blocks).max(-1, keepdims=True)
    byte = np.maximum(np.where(amax > 0, np.frexp(amax)[1] - 1 + 127, 0) - down, 1)
    scale = np.exp2(byte - 127.0)
    codes = (blocks / scale).astype(np.float32).astype(dtype).astype(np.float64)
    return np.moveaxis((codes * scale).reshape(v.shape), -1, axis)


WIDE = False


def mx_kscale(k):
    if not WIDE:
        return np.ones(k)
    levels = np.array([10, -10, 5, -5, 0])
    if k % 512:
        return np.exp2(np.random.permutation(np.resize(levels, k // 32))).repeat(32)
    a = np.empty((k // 512, 16))
    for p in range(k // 512):
        a[p, :8] = np.random.permutation(np.resize(levels, 8))
        for g in range(8):
            far = levels[np.abs(levels - a[p, g]) >= 10]
            a[p, g + 8] = far[np.random.randint(len(far))]
    return np.exp2(a.ravel()).repeat(32)


def f64(x):
    return np.asarray(x).astype(np.float64)


def striped8(idx):
    return np.asarray(idx).reshape(8, -1, 16).transpose(0, 2, 1).reshape(128, -1).astype(np.uint16)


def unstriped8(offs):
    return offs.reshape(8, 16, -1).transpose(0, 2, 1).reshape(8, -1).astype(np.int64)


def pick8(x, idx, run):
    r = np.arange(len(x))
    return x[r[:, None], idx[r % (8 * run) // run]]


E2M1 = np.array([0.0, 0.5, 1.0, 1.5, 2.0, 3.0, 4.0, 6.0, -0.0, -0.5, -1.0, -1.5, -2.0, -3.0, -4.0, -6.0])


def pack_weight(w, fmt):
    k, n = w.shape
    w = f64(np.asarray(w, np.float32).astype(ml_dtypes.bfloat16)).reshape(k // 32, 32, n)
    amax = np.abs(w).max(1)
    if fmt == "e4m3":
        byte = np.frexp(amax)[1] - 1 + 127 - 7
    else:
        mant, ex = np.frexp(amax / 6.0)
        byte = np.where(mant > 0.5, ex, ex - 1) + 127
    byte = np.clip(np.where(amax > 0, byte, 1), 1, 254)
    scaled = (w * np.exp2(127.0 - byte)[:, None, :]).reshape(k, n).astype(np.float32)
    by_word = np.ascontiguousarray(scaled.reshape(k // 512, 128, 4, n).transpose(0, 1, 3, 2))
    if fmt == "e4m3":
        words = by_word.astype(ml_dtypes.float8_e4m3fn).view(np.uint8)
    else:
        c = by_word.astype(ml_dtypes.float4_e2m1fn).view(np.uint8) & 0xF
        words = (c[..., 0::2] | (c[..., 1::2] << 4)).reshape(k // 512, 128, 2 * n)
    return np.ascontiguousarray(words), np.ascontiguousarray(byte.astype(np.uint8).reshape(k // 512, 16, n))


def unpack_weight(words, scales, fmt):
    g, _, n = scales.shape
    words = np.ascontiguousarray(words).reshape(g, 128, n, -1)
    if fmt == "e4m3":
        vals = words.view(ml_dtypes.float8_e4m3fn).astype(np.float64)
    else:
        nib = np.empty((g, 128, n, 4), np.uint8)
        nib[..., 0::2] = words & 0xF
        nib[..., 1::2] = words >> 4
        vals = E2M1[nib]
    vals = vals * np.repeat(np.exp2(scales.astype(np.float64) - 127.0), 8, axis=1)[..., None]
    return vals.transpose(0, 1, 3, 2).reshape(g * 512, n)


D, T, I, Q = 512, 1024, 512, 128


def setup_inputs():
    n = np.random.standard_normal
    idx = np.stack([np.random.permutation(T)[:I] for _ in range(8)])
    idx2 = np.stack([np.random.permutation(T)[:I] for _ in range(8)])
    idx3 = np.stack([np.random.permutation(T)[:I] for _ in range(8)])
    fd = mx_kscale(D)
    keysp = pack_weight(n((D, T)) / fd[:, None], "e2m1")
    return {
        "query": (n((D, Q)) * 1.0 / np.sqrt(D) * fd[:, None]).astype(np.float32),
        "keys_words": keysp[0],
        "keys_scales": keysp[1],
        "lam": (np.random.uniform(0.3, 0.7, (Q, 1))).astype(np.float32),
        "offs": striped8(idx),
        "offs2": striped8(idx2),
        "offs3": striped8(idx3),
    }


def reference(query, keys_words, keys_scales, lam, offs, offs2, offs3):
    idx = unstriped8(offs)
    idx2 = unstriped8(offs2)
    idx3 = unstriped8(offs3)
    keysu = unpack_weight(keys_words, keys_scales, "e2m1")
    queryq = mxq(f64(query), 0, "e4m3")
    a = queryq.T @ keysu
    f1 = np.zeros((Q, T))
    f1[np.arange(Q)[:, None], idx2[np.arange(Q) % 128 // 16]] = pick8(a, idx, 16)
    c1 = a + f1 * f64(lam)
    f2 = np.zeros((Q, T))
    f2[np.arange(Q)[:, None], idx2[np.arange(Q) % 128 // 16]] = pick8(c1, idx, 16)
    c2 = a + f2 * f64(lam)
    y = pick8(c2, idx3, 16)
    return y

@@ -1,0 +1,100 @@
+from contextlib import ExitStack
+
+import concourse.mybir as mybir
+
+D, T, I, Q = 512, 1024, 512, 128
+FLOPS = 2 * D * T * Q
+
+F32 = mybir.dt.float32
+BF16 = mybir.dt.bfloat16
+I32 = mybir.dt.int32
+U32 = mybir.dt.uint32
+U16 = mybir.dt.uint16
+U8 = mybir.dt.uint8
+FP8X4 = mybir.dt.float8_e4m3fn_x4
+FP4X4 = mybir.dt.float4_e2m1fn_x4
+MULT = mybir.AluOpType.mult
+ADD = mybir.AluOpType.add
+COPY = mybir.ActivationFunctionType.Copy
+
+P = 128
+PACK = 4
+N_TILE = 256
+HALF = I // 2
+HC = HALF // 16
+
+
+def tile_attend_samelinks_one_kernel(tc, query, keys_words, keys_scales, lam, offs, offs2, offs3, out):
+    nc = tc.nc
+    with ExitStack() as ctx:
+        keep = ctx.enter_context(tc.tile_pool(name="keep", bufs=1))
+        psum = ctx.enter_context(tc.psum_pool(name="psum", bufs=1))
+
+        k_scales = keep.tile([P, T], U8, name="k_scales", align_bytes=64)
+        nc.vector.memset(k_scales[:].bitcast(I32), 0)
+
+        q_raw = keep.tile([P, PACK, Q], F32, name="q_raw")
+        nc.sync.dma_start(q_raw[:], query.rearrange("(p j) q -> p j q", j=PACK))
+        k_words = keep.tile([P, 2 * T], U8, name="k_words", align_bytes=64)
+        nc.sync.dma_start(k_words[:].bitcast(I32), keys_words[0].bitcast(I32))
+        for quad in range(4):
+            nc.scalar.dma_start(
+                k_scales[32 * quad : 32 * quad + 4, :].bitcast(I32),
+                keys_scales[0, 4 * quad : 4 * quad + 4, :].bitcast(I32),
+            )
+        src_list = keep.tile([P, I // 16], U16, name="src_list")
+        nc.sync.dma_start(src_list[:], offs)
+        dst_list = keep.tile([P, I // 16], U16, name="dst_list")
+        nc.sync.dma_start(dst_list[:], offs2)
+        lam_col = keep.tile([P, 1], F32, name="lam_col")
+        nc.sync.dma_start(lam_col[:], lam)
+        out_list = keep.tile([P, I // 16], U16, name="out_list")
+        nc.sync.dma_start(out_list[:], offs3)
+
+        inflow = keep.tile([P, T], F32, name="inflow")
+        nc.vector.memset(inflow[:], 0.0)
+
+        q_bf = keep.tile([P, Q, PACK], BF16, name="q_bf", align_bytes=64)
+        nc.vector.tensor_copy(q_bf[:], q_raw[:].rearrange("p j q -> p q j"))
+        q_codes = keep.tile([P, Q], U32, name="q_codes", align_bytes=64)
+        q_scales = keep.tile([P, Q], U8, name="q_scales", align_bytes=64)
+        nc.vector.quantize_mx(
+            out=q_codes[:].bitcast(FP8X4), scales=q_scales[:], in_=q_bf[:].rearrange("p q j -> p (q j)")
+        )
+
+        a = keep.tile([P, T], F32, name="a")
+        for b in range(T // N_TILE):
+            cols = slice(b * N_TILE, (b + 1) * N_TILE)
+            bank = psum.tile([P, 512], F32, name="bank%d" % b)
+            nc.tensor.matmul_mx(
+                out=bank[:, 0:N_TILE],
+                lhsT=q_codes[:].bitcast(FP8X4),
+                lhsT_scale=q_scales[:],
+                rhs=k_words[:, 2 * cols.start : 2 * cols.stop].bitcast(FP4X4),
+                rhs_scale=k_scales[:, cols],
+                start=True,
+                stop=True,
+            )
+            if b % 2 == 0:
+                nc.scalar.copy(a[:, cols], bank[:, 0:N_TILE])
+            else:
+                nc.vector.tensor_copy(a[:, cols], bank[:, 0:N_TILE])
+
+        def look_up(table, offsets, name):
+            lo = keep.tile([P, HALF], F32, name=name + "_lo")
+            hi = keep.tile([P, HALF], F32, name=name + "_hi")
+            nc.vector.tensor_copy(lo[:], table[:].indirect(offsets[:, 0:HC]))
+            nc.scalar.activation(hi[:], table[:].indirect(offsets[:, HC : 2 * HC]), COPY)
+            return lo, hi
+
+        carried = a
+        for step in range(2):
+            lo, hi = look_up(carried, src_list, "sent%d" % step)
+            nc.vector.tensor_copy(inflow[:].indirect(dst_list[:, 0:HC]), lo[:])
+            nc.vector.tensor_copy(inflow[:].indirect(dst_list[:, HC : 2 * HC]), hi[:])
+            carried = keep.tile([P, T], F32, name="c%d" % (step + 1))
+            nc.vector.scalar_tensor_tensor(carried[:], inflow[:], lam_col[:], a[:], MULT, ADD)
+
+        lo, hi = look_up(carried, out_list, "result")
+        nc.sync.dma_start(out[:, 0:HALF], lo[:])
+        nc.scalar.dma_start(out[:, HALF:I], hi[:])

@@ -19,7 +19,8 @@ COPY = mybir.ActivationFunctionType.Copy
 
 P = 128
 PACK = 4
-N_TILE = 256
+CHUNKS = (512, 256, 128, 128)
+VECTOR_COLS = 704
 HALF = I // 2
 HC = HALF // 16
 
@@ -42,17 +43,19 @@ def tile_attend_samelinks_one_kernel(tc, query, keys_words, keys_scales, lam, of
                 k_scales[32 * quad : 32 * quad + 4, :].bitcast(I32),
                 keys_scales[0, 4 * quad : 4 * quad + 4, :].bitcast(I32),
             )
+        lam_col = keep.tile([P, 1], F32, name="lam_col")
+        nc.sync.dma_start(lam_col[:], lam)
         src_list = keep.tile([P, I // 16], U16, name="src_list")
         nc.sync.dma_start(src_list[:], offs)
         dst_list = keep.tile([P, I // 16], U16, name="dst_list")
         nc.sync.dma_start(dst_list[:], offs2)
-        lam_col = keep.tile([P, 1], F32, name="lam_col")
-        nc.sync.dma_start(lam_col[:], lam)
         out_list = keep.tile([P, I // 16], U16, name="out_list")
         nc.sync.dma_start(out_list[:], offs3)
 
         inflow = keep.tile([P, T], F32, name="inflow")
         nc.vector.memset(inflow[:], 0.0)
+        lam_wide = keep.tile([P, I], F32, name="lam_wide")
+        nc.scalar.copy(lam_wide[:], lam_col[:].to_broadcast([P, I]))
 
         q_bf = keep.tile([P, Q, PACK], BF16, name="q_bf", align_bytes=64)
         nc.vector.tensor_copy(q_bf[:], q_raw[:].rearrange("p j q -> p q j"))
@@ -63,11 +66,15 @@ def tile_attend_samelinks_one_kernel(tc, query, keys_words, keys_scales, lam, of
         )
 
         a = keep.tile([P, T], F32, name="a")
-        for b in range(T // N_TILE):
-            cols = slice(b * N_TILE, (b + 1) * N_TILE)
+        banks = []
+        first = 0
+        for b, width in enumerate(CHUNKS):
+            cols = slice(first, first + width)
+            first += width
             bank = psum.tile([P, 512], F32, name="bank%d" % b)
+            banks.append((bank, cols))
             nc.tensor.matmul_mx(
-                out=bank[:, 0:N_TILE],
+                out=bank[:, 0:width],
                 lhsT=q_codes[:].bitcast(FP8X4),
                 lhsT_scale=q_scales[:],
                 rhs=k_words[:, 2 * cols.start : 2 * cols.stop].bitcast(FP4X4),
@@ -75,26 +82,30 @@ def tile_attend_samelinks_one_kernel(tc, query, keys_words, keys_scales, lam, of
                 start=True,
                 stop=True,
             )
-            if b % 2 == 0:
-                nc.scalar.copy(a[:, cols], bank[:, 0:N_TILE])
+            if b in (0, 3):
+                nc.scalar.copy(a[:, cols], bank[:, 0:width])
             else:
-                nc.vector.tensor_copy(a[:, cols], bank[:, 0:N_TILE])
+                nc.vector.tensor_copy(a[:, cols], bank[:, 0:width])
 
-        def look_up(table, offsets, name):
-            lo = keep.tile([P, HALF], F32, name=name + "_lo")
-            hi = keep.tile([P, HALF], F32, name=name + "_hi")
-            nc.vector.tensor_copy(lo[:], table[:].indirect(offsets[:, 0:HC]))
-            nc.scalar.activation(hi[:], table[:].indirect(offsets[:, HC : 2 * HC]), COPY)
-            return lo, hi
+        def look_up(table, offsets, lo, hi):
+            nc.vector.tensor_copy(lo, table[:].indirect(offsets[:, 0:HC]))
+            nc.scalar.activation(hi, table[:].indirect(offsets[:, HC : 2 * HC]), COPY)
 
         carried = a
         for step in range(2):
-            lo, hi = look_up(carried, src_list, "sent%d" % step)
-            nc.vector.tensor_copy(inflow[:].indirect(dst_list[:, 0:HC]), lo[:])
-            nc.vector.tensor_copy(inflow[:].indirect(dst_list[:, HC : 2 * HC]), hi[:])
+            sent = keep.tile([P, I], F32, name="sent%d" % step)
+            look_up(carried, src_list, sent[:, 0:HALF], sent[:, HALF:I])
+            nc.vector.tensor_tensor(inflow[:].indirect(dst_list[:]), sent[:], lam_wide[:], MULT)
             carried = keep.tile([P, T], F32, name="c%d" % (step + 1))
-            nc.vector.scalar_tensor_tensor(carried[:], inflow[:], lam_col[:], a[:], MULT, ADD)
+            for bank, cols in banks[:2]:
+                stop = min(cols.stop, VECTOR_COLS)
+                mine = slice(cols.start, stop)
+                nc.vector.tensor_tensor(carried[:, mine], inflow[:, mine], bank[:, 0 : stop - cols.start], ADD)
+            rest = slice(VECTOR_COLS, T)
+            nc.gpsimd.tensor_tensor(carried[:, rest], inflow[:, rest], a[:, rest], ADD)
 
-        lo, hi = look_up(carried, out_list, "result")
+        lo = keep.tile([P, HALF], F32, name="result_lo")
+        hi = keep.tile([P, HALF], F32, name="result_hi")
+        look_up(carried, out_list, lo[:], hi[:])
         nc.sync.dma_start(out[:, 0:HALF], lo[:])
         nc.scalar.dma_start(out[:, HALF:I], hi[:])

@@ -21,6 +21,7 @@ P = 128
 PACK = 4
 CHUNKS = (512, 256, 128, 128)
 VECTOR_COLS = 704
+CAST_SPLIT = 22
 HALF = I // 2
 HC = HALF // 16
 
@@ -39,7 +40,7 @@ def tile_attend_samelinks_one_kernel(tc, query, keys_words, keys_scales, lam, of
         k_words = keep.tile([P, 2 * T], U8, name="k_words", align_bytes=64)
         nc.sync.dma_start(k_words[:].bitcast(I32), keys_words[0].bitcast(I32))
         for quad in range(4):
-            nc.scalar.dma_start(
+            nc.sync.dma_start(
                 k_scales[32 * quad : 32 * quad + 4, :].bitcast(I32),
                 keys_scales[0, 4 * quad : 4 * quad + 4, :].bitcast(I32),
             )
@@ -54,16 +55,20 @@ def tile_attend_samelinks_one_kernel(tc, query, keys_words, keys_scales, lam, of
 
         inflow = keep.tile([P, T], F32, name="inflow")
         nc.vector.memset(inflow[:], 0.0)
-        lam_wide = keep.tile([P, I], F32, name="lam_wide")
-        nc.scalar.copy(lam_wide[:], lam_col[:].to_broadcast([P, I]))
 
-        q_bf = keep.tile([P, Q, PACK], BF16, name="q_bf", align_bytes=64)
-        nc.vector.tensor_copy(q_bf[:], q_raw[:].rearrange("p j q -> p q j"))
+        q_bf = keep.tile([P, Q, PACK], BF16, name="q_bf", tag="reused", align_bytes=64)
+        by_fours = q_bf[:].rearrange("p (c i) j -> p c j i", i=4)
+        raw_by_fours = q_raw[:].rearrange("p j (c i) -> p c j i", i=4)
+        nc.vector.tensor_copy(by_fours[:, 0:CAST_SPLIT], raw_by_fours[:, 0:CAST_SPLIT])
+        nc.scalar.copy(by_fours[:, CAST_SPLIT:], raw_by_fours[:, CAST_SPLIT:])
         q_codes = keep.tile([P, Q], U32, name="q_codes", align_bytes=64)
         q_scales = keep.tile([P, Q], U8, name="q_scales", align_bytes=64)
         nc.vector.quantize_mx(
             out=q_codes[:].bitcast(FP8X4), scales=q_scales[:], in_=q_bf[:].rearrange("p q j -> p (q j)")
         )
+
+        lam_wide = keep.tile([P, I], F32, name="lam_wide", tag="reused", align_bytes=64)
+        nc.gpsimd.tensor_scalar(lam_wide[:], lam_col[:].to_broadcast([P, I]), 1.0, 0.0, MULT, ADD)
 
         a = keep.tile([P, T], F32, name="a")
         banks = []

@@ -37,13 +37,16 @@ def tile_attend_samelinks_one_kernel(tc, query, keys_words, keys_scales, lam, of
 
         q_raw = keep.tile([P, PACK, Q], F32, name="q_raw")
         nc.sync.dma_start(q_raw[:], query.rearrange("(p j) q -> p j q", j=PACK))
-        k_words = keep.tile([P, 2 * T], U8, name="k_words", align_bytes=64)
-        nc.sync.dma_start(k_words[:].bitcast(I32), keys_words[0].bitcast(I32))
         for quad in range(4):
             nc.sync.dma_start(
                 k_scales[32 * quad : 32 * quad + 4, :].bitcast(I32),
                 keys_scales[0, 4 * quad : 4 * quad + 4, :].bitcast(I32),
             )
+        k_halves = []
+        for h in range(2):
+            k_half = keep.tile([P, T], U8, name="k_words%d" % h, align_bytes=64)
+            nc.sync.dma_start(k_half[:].bitcast(I32), keys_words[0, :, h * T : (h + 1) * T].bitcast(I32))
+            k_halves.append(k_half)
         lam_col = keep.tile([P, 1], F32, name="lam_col")
         nc.sync.dma_start(lam_col[:], lam)
         src_list = keep.tile([P, I // 16], U16, name="src_list")
@@ -82,7 +85,7 @@ def tile_attend_samelinks_one_kernel(tc, query, keys_words, keys_scales, lam, of
                 out=bank[:, 0:width],
                 lhsT=q_codes[:].bitcast(FP8X4),
                 lhsT_scale=q_scales[:],
-                rhs=k_words[:, 2 * cols.start : 2 * cols.stop].bitcast(FP4X4),
+                rhs=k_halves[2 * cols.start // T][:, 2 * cols.start % T : 2 * cols.start % T + 2 * width].bitcast(FP4X4),
                 rhs_scale=k_scales[:, cols],
                 start=True,
                 stop=True,

from contextlib import ExitStack

import concourse.mybir as mybir

D, T, I, Q = 512, 1024, 512, 128
FLOPS = 2 * D * T * Q

F32 = mybir.dt.float32
BF16 = mybir.dt.bfloat16
I32 = mybir.dt.int32
U32 = mybir.dt.uint32
U16 = mybir.dt.uint16
U8 = mybir.dt.uint8
FP8X4 = mybir.dt.float8_e4m3fn_x4
FP4X4 = mybir.dt.float4_e2m1fn_x4
MULT = mybir.AluOpType.mult
ADD = mybir.AluOpType.add
COPY = mybir.ActivationFunctionType.Copy

P = 128
PACK = 4
CHUNKS = (512, 256, 128, 128)
VECTOR_COLS = 704
CAST_SPLIT = 22
HALF = I // 2
HC = HALF // 16


def tile_attend_samelinks_one_kernel(tc, query, keys_words, keys_scales, lam, offs, offs2, offs3, out):
    nc = tc.nc
    with ExitStack() as ctx:
        keep = ctx.enter_context(tc.tile_pool(name="keep", bufs=1))
        psum = ctx.enter_context(tc.psum_pool(name="psum", bufs=1))

        k_scales = keep.tile([P, T], U8, name="k_scales", align_bytes=64)
        nc.vector.memset(k_scales[:].bitcast(I32), 0)

        q_raw = keep.tile([P, PACK, Q], F32, name="q_raw")
        nc.sync.dma_start(q_raw[:], query.rearrange("(p j) q -> p j q", j=PACK))
        for quad in range(4):
            nc.sync.dma_start(
                k_scales[32 * quad : 32 * quad + 4, :].bitcast(I32),
                keys_scales[0, 4 * quad : 4 * quad + 4, :].bitcast(I32),
            )
        k_halves = []
        for h in range(2):
            k_half = keep.tile([P, T], U8, name="k_words%d" % h, align_bytes=64)
            nc.sync.dma_start(k_half[:].bitcast(I32), keys_words[0, :, h * T : (h + 1) * T].bitcast(I32))
            k_halves.append(k_half)
        lam_col = keep.tile([P, 1], F32, name="lam_col")
        nc.sync.dma_start(lam_col[:], lam)
        src_list = keep.tile([P, I // 16], U16, name="src_list")
        nc.sync.dma_start(src_list[:], offs)
        dst_list = keep.tile([P, I // 16], U16, name="dst_list")
        nc.sync.dma_start(dst_list[:], offs2)
        out_list = keep.tile([P, I // 16], U16, name="out_list")
        nc.sync.dma_start(out_list[:], offs3)

        inflow = keep.tile([P, T], F32, name="inflow")
        nc.vector.memset(inflow[:], 0.0)

        q_bf = keep.tile([P, Q, PACK], BF16, name="q_bf", tag="reused", align_bytes=64)
        by_fours = q_bf[:].rearrange("p (c i) j -> p c j i", i=4)
        raw_by_fours = q_raw[:].rearrange("p j (c i) -> p c j i", i=4)
        nc.vector.tensor_copy(by_fours[:, 0:CAST_SPLIT], raw_by_fours[:, 0:CAST_SPLIT])
        nc.scalar.copy(by_fours[:, CAST_SPLIT:], raw_by_fours[:, CAST_SPLIT:])
        q_codes = keep.tile([P, Q], U32, name="q_codes", align_bytes=64)
        q_scales = keep.tile([P, Q], U8, name="q_scales", align_bytes=64)
        nc.vector.quantize_mx(
            out=q_codes[:].bitcast(FP8X4), scales=q_scales[:], in_=q_bf[:].rearrange("p q j -> p (q j)")
        )

        lam_wide = keep.tile([P, I], F32, name="lam_wide", tag="reused", align_bytes=64)
        nc.gpsimd.tensor_scalar(lam_wide[:], lam_col[:].to_broadcast([P, I]), 1.0, 0.0, MULT, ADD)

        a = keep.tile([P, T], F32, name="a")
        banks = []
        first = 0
        for b, width in enumerate(CHUNKS):
            cols = slice(first, first + width)
            first += width
            bank = psum.tile([P, 512], F32, name="bank%d" % b)
            banks.append((bank, cols))
            nc.tensor.matmul_mx(
                out=bank[:, 0:width],
                lhsT=q_codes[:].bitcast(FP8X4),
                lhsT_scale=q_scales[:],
                rhs=k_halves[2 * cols.start // T][:, 2 * cols.start % T : 2 * cols.start % T + 2 * width].bitcast(FP4X4),
                rhs_scale=k_scales[:, cols],
                start=True,
                stop=True,
            )
            if b in (0, 3):
                nc.scalar.copy(a[:, cols], bank[:, 0:width])
            else:
                nc.vector.tensor_copy(a[:, cols], bank[:, 0:width])

        def look_up(table, offsets, lo, hi):
            nc.vector.tensor_copy(lo, table[:].indirect(offsets[:, 0:HC]))
            nc.scalar.activation(hi, table[:].indirect(offsets[:, HC : 2 * HC]), COPY)

        carried = a
        for step in range(2):
            sent = keep.tile([P, I], F32, name="sent%d" % step)
            look_up(carried, src_list, sent[:, 0:HALF], sent[:, HALF:I])
            nc.vector.tensor_tensor(inflow[:].indirect(dst_list[:]), sent[:], lam_wide[:], MULT)
            carried = keep.tile([P, T], F32, name="c%d" % (step + 1))
            for bank, cols in banks[:2]:
                stop = min(cols.stop, VECTOR_COLS)
                mine = slice(cols.start, stop)
                nc.vector.tensor_tensor(carried[:, mine], inflow[:, mine], bank[:, 0 : stop - cols.start], ADD)
            rest = slice(VECTOR_COLS, T)
            nc.gpsimd.tensor_tensor(carried[:, rest], inflow[:, rest], a[:, rest], ADD)

        lo = keep.tile([P, HALF], F32, name="result_lo")
        hi = keep.tile([P, HALF], F32, name="result_hi")
        look_up(carried, out_list, lo[:], hi[:])
        nc.sync.dma_start(out[:, 0:HALF], lo[:])
        nc.scalar.dma_start(out[:, HALF:I], hi[:])
